import numpy as np
import ml_dtypes

BF16 = ml_dtypes.bfloat16


def bf(x):
    return np.asarray(x, np.float32).astype(BF16)


def f32(x):
    return np.asarray(x, np.float32)


def f64(x):
    return np.asarray(x).astype(np.float64)


def striped(idx):
    return np.tile(idx.reshape(-1, 16).T, (8, 1))


S, K, M, N, E, Q, O = 256, 128, 128, 256, 2, 128, 256


def gelu_tanh(v):
    return 0.5 * v * (1.0 + np.tanh(np.sqrt(2.0 / np.pi) * (v + 0.044715 * v**3)))


def setup_inputs():
    return {"base": bf(np.random.standard_normal((M, S))), "x": bf(np.random.standard_normal((K, N))), "w": bf(1.2 * np.random.standard_normal((E, K, M)) / np.sqrt(K)), "w2": bf(np.random.standard_normal((M, O)) / np.sqrt(2 * M)), "b": f32(0.5 * np.random.standard_normal((O, 1))), "offs": striped(np.random.permutation(S))}


def reference(base, x, w, w2, b, offs):
    idx = offs[:16].T.reshape(-1)
    z = f64(base).copy()
    for e in range(E):
        z[:, idx[e * Q : (e + 1) * Q]] += f64(w)[e].T @ f64(x)[:, e * Q : (e + 1) * Q]
    y = f64(w2).T @ z
    return gelu_tanh(y + f64(b))

@@ -1,0 +1,67 @@
+import concourse.mybir as mybir
+from concourse.masks import make_identity
+
+BF16 = mybir.dt.bfloat16
+F32 = mybir.dt.float32
+U16 = mybir.dt.uint16
+GELU = mybir.ActivationFunctionType.Gelu_apprx_tanh
+
+P = 128
+S = 256
+E = 2
+O = 256
+O_BLOCKS = O // P
+PIECE_COLUMNS = P // 16
+
+FLOPS = 2 * P * P * E * P + 2 * P * O * S
+
+
+def tile_rows_thenproj_gelu_kernel(tc, base, x, w, w2, b, offs, out):
+    nc = tc.nc
+    with (
+        tc.tile_pool(name="held", bufs=1) as held,
+        tc.psum_pool(name="psum", bufs=1) as psum,
+    ):
+        base_sb = held.tile([P, S], BF16)
+        x_sb = held.tile([P, E * P], BF16)
+        w_sb = held.tile([P, E, P], BF16)
+        w2_sb = held.tile([P, O], BF16)
+        bias_sb = held.tile([P, O_BLOCKS], F32)
+        offs_sb = held.tile([P, E * PIECE_COLUMNS], U16)
+        nc.sync.dma_start(base_sb[:], base)
+        nc.sync.dma_start(offs_sb[:], offs)
+        nc.scalar.dma_start(x_sb[:], x)
+        nc.scalar.dma_start(w_sb[:], w.rearrange("e k m -> k e m"))
+        nc.sync.dma_start(w2_sb[:], w2)
+        nc.sync.dma_start(bias_sb[:], b.rearrange("(a p) o -> p (a o)", p=P))
+
+        identity = held.tile([P, P], BF16)
+        make_identity(nc, identity[:])
+
+        zero = held.tile([P, 1], F32)
+        gelu_of_zero = held.tile([P, 1], F32)
+        nc.vector.memset(zero[:], 0.0)
+        nc.scalar.activation(gelu_of_zero[:], zero[:], GELU)
+
+        z = psum.tile([P, S], F32)
+        nc.tensor.matmul(z[:], identity[:], base_sb[:], start=True, stop=False)
+        for e in range(E):
+            piece = offs_sb[:, e * PIECE_COLUMNS : (e + 1) * PIECE_COLUMNS]
+            nc.tensor.matmul(
+                z[:].indirect(piece),
+                w_sb[:, e, :],
+                x_sb[:, e * P : (e + 1) * P],
+                start=False,
+                stop=(e == E - 1),
+            )
+
+        z_sb = held.tile([P, S], BF16)
+        nc.vector.tensor_copy(z_sb[:], z[:])
+
+        for a in range(O_BLOCKS):
+            rows = slice(a * P, (a + 1) * P)
+            y = psum.tile([P, S], F32, name=f"y{a}")
+            nc.tensor.matmul(y[:], w2_sb[:, rows], z_sb[:], start=True, stop=True)
+            out_sb = held.tile([P, S], F32, name=f"out{a}")
+            nc.scalar.activation(out_sb[:], y[:], GELU, bias=bias_sb[:, a : a + 1])
+            nc.sync.dma_start(out[rows, :], out_sb[:])

@@ -11,6 +11,8 @@ S = 256
 E = 2
 O = 256
 O_BLOCKS = O // P
+HALVES = 2
+HALF = S // HALVES
 PIECE_COLUMNS = P // 16
 
 FLOPS = 2 * P * P * E * P + 2 * P * O * S
@@ -56,12 +58,13 @@ def tile_rows_thenproj_gelu_kernel(tc, base, x, w, w2, b, offs, out):
             )
 
         z_sb = held.tile([P, S], BF16)
-        nc.vector.tensor_copy(z_sb[:], z[:])
-
-        for a in range(O_BLOCKS):
-            rows = slice(a * P, (a + 1) * P)
-            y = psum.tile([P, S], F32, name=f"y{a}")
-            nc.tensor.matmul(y[:], w2_sb[:, rows], z_sb[:], start=True, stop=True)
-            out_sb = held.tile([P, S], F32, name=f"out{a}")
-            nc.scalar.activation(out_sb[:], y[:], GELU, bias=bias_sb[:, a : a + 1])
-            nc.sync.dma_start(out[rows, :], out_sb[:])
+        out_blocks = out.rearrange("(a p) i -> p a i", p=P)
+        for h in range(HALVES):
+            columns = slice(h * HALF, (h + 1) * HALF)
+            nc.vector.tensor_copy(z_sb[:, columns], z[:, columns])
+            out_sb = held.tile([P, O_BLOCKS, HALF], F32, name=f"out{h}")
+            for a in range(O_BLOCKS):
+                y = psum.tile([P, HALF], F32, name=f"y{h}{a}")
+                nc.tensor.matmul(y[:], w2_sb[:, a * P : (a + 1) * P], z_sb[:, columns], start=True, stop=True)
+                nc.scalar.activation(out_sb[:, a, :], y[:], GELU, bias=bias_sb[:, a : a + 1])
+            nc.sync.dma_start(out_blocks[:, :, columns], out_sb[:])

@@ -15,6 +15,9 @@ HALVES = 2
 HALF = S // HALVES
 PIECE_COLUMNS = P // 16
 
+WARM_COLUMNS = 256
+WARM_MATMULS = 6
+
 FLOPS = 2 * P * P * E * P + 2 * P * O * S
 
 
@@ -36,6 +39,11 @@ def tile_rows_thenproj_gelu_kernel(tc, base, x, w, w2, b, offs, out):
         nc.scalar.dma_start(w_sb[:], w.rearrange("e k m -> k e m"))
         nc.sync.dma_start(w2_sb[:], w2)
         nc.sync.dma_start(bias_sb[:], b.rearrange("(a p) o -> p (a o)", p=P))
+        zeros = held.tile([P, WARM_COLUMNS], BF16)
+        nc.vector.memset(zeros[:], 0.0)
+        warm = psum.tile([P, WARM_COLUMNS], F32)
+        for i in range(WARM_MATMULS):
+            nc.tensor.matmul(warm[:], zeros[:, :P], zeros[:], start=True, stop=True)
 
         identity = held.tile([P, P], BF16)
         make_identity(nc, identity[:])

import concourse.mybir as mybir
from concourse.masks import make_identity

BF16 = mybir.dt.bfloat16
F32 = mybir.dt.float32
U16 = mybir.dt.uint16
GELU = mybir.ActivationFunctionType.Gelu_apprx_tanh

P = 128
S = 256
E = 2
O = 256
O_BLOCKS = O // P
HALVES = 2
HALF = S // HALVES
PIECE_COLUMNS = P // 16

WARM_COLUMNS = 256
WARM_MATMULS = 6

FLOPS = 2 * P * P * E * P + 2 * P * O * S


def tile_rows_thenproj_gelu_kernel(tc, base, x, w, w2, b, offs, out):
    nc = tc.nc
    with (
        tc.tile_pool(name="held", bufs=1) as held,
        tc.psum_pool(name="psum", bufs=1) as psum,
    ):
        base_sb = held.tile([P, S], BF16)
        x_sb = held.tile([P, E * P], BF16)
        w_sb = held.tile([P, E, P], BF16)
        w2_sb = held.tile([P, O], BF16)
        bias_sb = held.tile([P, O_BLOCKS], F32)
        offs_sb = held.tile([P, E * PIECE_COLUMNS], U16)
        nc.sync.dma_start(base_sb[:], base)
        nc.sync.dma_start(offs_sb[:], offs)
        nc.scalar.dma_start(x_sb[:], x)
        nc.scalar.dma_start(w_sb[:], w.rearrange("e k m -> k e m"))
        nc.sync.dma_start(w2_sb[:], w2)
        nc.sync.dma_start(bias_sb[:], b.rearrange("(a p) o -> p (a o)", p=P))
        zeros = held.tile([P, WARM_COLUMNS], BF16)
        nc.vector.memset(zeros[:], 0.0)
        warm = psum.tile([P, WARM_COLUMNS], F32)
        for i in range(WARM_MATMULS):
            nc.tensor.matmul(warm[:], zeros[:, :P], zeros[:], start=True, stop=True)

        identity = held.tile([P, P], BF16)
        make_identity(nc, identity[:])

        zero = held.tile([P, 1], F32)
        gelu_of_zero = held.tile([P, 1], F32)
        nc.vector.memset(zero[:], 0.0)
        nc.scalar.activation(gelu_of_zero[:], zero[:], GELU)

        z = psum.tile([P, S], F32)
        nc.tensor.matmul(z[:], identity[:], base_sb[:], start=True, stop=False)
        for e in range(E):
            piece = offs_sb[:, e * PIECE_COLUMNS : (e + 1) * PIECE_COLUMNS]
            nc.tensor.matmul(
                z[:].indirect(piece),
                w_sb[:, e, :],
                x_sb[:, e * P : (e + 1) * P],
                start=False,
                stop=(e == E - 1),
            )

        z_sb = held.tile([P, S], BF16)
        out_blocks = out.rearrange("(a p) i -> p a i", p=P)
        for h in range(HALVES):
            columns = slice(h * HALF, (h + 1) * HALF)
            nc.vector.tensor_copy(z_sb[:, columns], z[:, columns])
            out_sb = held.tile([P, O_BLOCKS, HALF], F32, name=f"out{h}")
            for a in range(O_BLOCKS):
                y = psum.tile([P, HALF], F32, name=f"y{h}{a}")
                nc.tensor.matmul(y[:], w2_sb[:, a * P : (a + 1) * P], z_sb[:, columns], start=True, stop=True)
                nc.scalar.activation(out_sb[:, a, :], y[:], GELU, bias=bias_sb[:, a : a + 1])
            nc.sync.dma_start(out_blocks[:, :, columns], out_sb[:])
